import numpy as np
import ml_dtypes


def mxq(x, axis, fmt="e4m3"):
    dtype, down = {"e4m3": (ml_dtypes.float8_e4m3fn, 7), "e5m2": (ml_dtypes.float8_e5m2, 14)}[fmt]
    v = np.moveaxis(np.asarray(x, np.float32).astype(ml_dtypes.bfloat16).astype(np.float64), axis, -1)
    blocks = v.reshape(v.shape[:-1] + (-1, 32))
    amax = np.abs(blocks).max(-1, keepdims=True)
    byte = np.maximum(np.where(amax > 0, np.frexp(amax)[1] - 1 + 127, 0) - down, 1)
    scale = np.exp2(byte - 127.0)
    codes = (blocks / scale).astype(np.float32).astype(dtype).astype(np.float64)
    return np.moveaxis((codes * scale).reshape(v.shape), -1, axis)


WIDE = False


def mx_kscale(k):
    if not WIDE:
        return np.ones(k)
    levels = np.array([10, -10, 5, -5, 0])
    if k % 512:
        return np.exp2(np.random.permutation(np.resize(levels, k // 32))).repeat(32)
    a = np.empty((k // 512, 16))
    for p in range(k // 512):
        a[p, :8] = np.random.permutation(np.resize(levels, 8))
        for g in range(8):
            far = levels[np.abs(levels - a[p, g]) >= 10]
            a[p, g + 8] = far[np.random.randint(len(far))]
    return np.exp2(a.ravel()).repeat(32)


def f64(x):
    return np.asarray(x).astype(np.float64)


def striped(idx):
    return np.tile(np.asarray(idx).reshape(-1, 16).T, (8, 1)).astype(np.uint16)


def unstriped(offs):
    return offs[:16].T.reshape(-1).astype(np.int64)


E2M1 = np.array([0.0, 0.5, 1.0, 1.5, 2.0, 3.0, 4.0, 6.0, -0.0, -0.5, -1.0, -1.5, -2.0, -3.0, -4.0, -6.0])


def pack_weight(w, fmt):
    k, n = w.shape
    w = f64(np.asarray(w, np.float32).astype(ml_dtypes.bfloat16)).reshape(k // 32, 32, n)
    amax = np.abs(w).max(1)
    if fmt == "e4m3":
        byte = np.frexp(amax)[1] - 1 + 127 - 7
    else:
        mant, ex = np.frexp(amax / 6.0)
        byte = np.where(mant > 0.5, ex, ex - 1) + 127
    byte = np.clip(np.where(amax > 0, byte, 1), 1, 254)
    scaled = (w * np.exp2(127.0 - byte)[:, None, :]).reshape(k, n).astype(np.float32)
    by_word = np.ascontiguousarray(scaled.reshape(k // 512, 128, 4, n).transpose(0, 1, 3, 2))
    if fmt == "e4m3":
        words = by_word.astype(ml_dtypes.float8_e4m3fn).view(np.uint8)
    else:
        c = by_word.astype(ml_dtypes.float4_e2m1fn).view(np.uint8) & 0xF
        words = (c[..., 0::2] | (c[..., 1::2] << 4)).reshape(k // 512, 128, 2 * n)
    return np.ascontiguousarray(words), np.ascontiguousarray(byte.astype(np.uint8).reshape(k // 512, 16, n))


def unpack_weight(words, scales, fmt):
    g, _, n = scales.shape
    words = np.ascontiguousarray(words).reshape(g, 128, n, -1)
    if fmt == "e4m3":
        vals = words.view(ml_dtypes.float8_e4m3fn).astype(np.float64)
    else:
        nib = np.empty((g, 128, n, 4), np.uint8)
        nib[..., 0::2] = words & 0xF
        nib[..., 1::2] = words >> 4
        vals = E2M1[nib]
    vals = vals * np.repeat(np.exp2(scales.astype(np.float64) - 127.0), 8, axis=1)[..., None]
    return vals.transpose(0, 1, 3, 2).reshape(g * 512, n)


def bf(x):
    return np.asarray(x, np.float32).astype(ml_dtypes.bfloat16)


def planes(Y):
    r, m = Y.shape
    b = f64(bf(Y)).reshape(r // 32, 32, m)
    amax = np.abs(b).max(1)
    byte = np.clip(np.where(amax > 0, np.frexp(amax)[1] - 1 + 127 - 7, 1), 1, 254)
    codes = (b * np.exp2(127.0 - byte)[:, None, :]).reshape(r, m).astype(np.float32).astype(ml_dtypes.float8_e4m3fn).view(np.uint8)
    words = codes.reshape(r // 512, 128, 4, m).transpose(0, 1, 3, 2)
    return np.ascontiguousarray(words), np.ascontiguousarray(byte.astype(np.uint8).reshape(r // 512, 16, m))


B, N, T, D, NQ = 1, 512, 2048, 512, 512
DV = 512


def sgn(shape):
    return np.random.uniform(0.5, 2.0, shape) * np.where(np.random.standard_normal(shape) < 0, -1.0, 1.0)


def setup_inputs():
    n = np.random.standard_normal
    idx = np.random.permutation(T)[:B * N]
    s = mx_kscale(D)[:, None]
    u = mx_kscale(N)
    ut = np.ones(T)
    ut[idx] = u
    kp = pack_weight(n((D, T)) / s, "e4m3")
    return {
        "qT": (n((B, D, NQ)) * s * (1.00 / np.sqrt(D))).astype(np.float32),
        "k_words": kp[0],
        "k_scales": kp[1],
        "vT": (n((DV, T)) / ut).astype(np.float32),
        "ls": (np.random.uniform(7.0, 7.6, (B, 1, NQ))).astype(np.float32),
        "us": (sgn((B, N, 1)) * u[:, None]).astype(np.float32),
        "offs": striped(idx),
    }


def reference(qT, k_words, k_scales, vT, ls, us, offs):
    idx = unstriped(offs)
    pick = lambda x, which: x[:, which].reshape(x.shape[0], B, -1).transpose(1, 0, 2)
    k = unpack_weight(k_words, k_scales, "e4m3")
    kg = pick(k, idx)
    qq = mxq(f64(qT), 1, "e4m3")
    a = kg.transpose(0, 2, 1) @ qq
    y = np.exp(a - f64(ls)) * f64(us)
    wq = mxq(y, 1, "e4m3")
    o = mxq(pick(f64(vT), idx).transpose(0, 2, 1), 1, "e4m3").transpose(0, 2, 1) @ wq
    Y = o[0]
    words, scales = planes(Y)
    return Y, words, scales

@@ -1,0 +1,170 @@
+from contextlib import ExitStack
+
+import concourse.mybir as mybir
+from concourse.masks import make_identity
+
+F32 = mybir.dt.float32
+BF16 = mybir.dt.bfloat16
+I32 = mybir.dt.int32
+U32 = mybir.dt.uint32
+U16 = mybir.dt.uint16
+U8 = mybir.dt.uint8
+FP8X4 = mybir.dt.float8_e4m3fn_x4
+ACT = mybir.ActivationFunctionType
+ALU = mybir.AluOpType
+
+P = 128
+PACK = 4
+SLOTS = 512
+TOKENS = 2048
+QUERIES = 512
+HALF = QUERIES // 2
+BLOCKS = QUERIES // P
+
+FLOPS = 2 * 2 * 512 * 512 * 512
+
+
+def tile_attend_plo_lse_topk_kernel(tc, qT, k_words, k_scales, vT, ls, us, offs, out_0, out_1, out_2):
+    nc = tc.nc
+    with ExitStack() as ctx:
+        sb = ctx.enter_context(tc.tile_pool(name="sb", bufs=1))
+        acc = ctx.enter_context(tc.psum_pool(name="acc", bufs=1))
+        turn = ctx.enter_context(tc.psum_pool(name="turn", bufs=3))
+
+        def tile(shape, dtype, name, tag=None):
+            return sb.tile(shape, dtype, name=name, tag=tag or name, align_bytes=64)
+
+        def quantize(codes, scales, values):
+            nc.vector.quantize_mx(out=codes.bitcast(FP8X4), scales=scales, in_=values)
+
+        def product(out, lhs_codes, lhs_scales, rhs_codes, rhs_scales):
+            nc.tensor.matmul_mx(out=out, lhsT=lhs_codes.bitcast(FP8X4), lhsT_scale=lhs_scales,
+                                rhs=rhs_codes.bitcast(FP8X4), rhs_scale=rhs_scales, start=True, stop=True)
+
+        offsets = sb.tile([P, SLOTS // 16], U16, name="offsets")
+        nc.sync.dma_start(offsets[:], offs)
+
+        key_scale_pool = tile([P, TOKENS], U8, "key_scale_pool")
+        nc.vector.memset(key_scale_pool[:].bitcast(I32), 0)
+        lse_rows = tile([P, P], F32, "lse_rows")
+        nc.vector.memset(lse_rows[:], 0.0)
+
+        key_word_pool = tile([P, TOKENS], I32, "key_word_pool")
+        nc.sync.dma_start(key_word_pool[:], k_words[0].rearrange("p n r -> p (n r)").bitcast(I32))
+        for quad in range(4):
+            nc.scalar.dma_start(key_scale_pool[32 * quad : 32 * quad + 4, :].bitcast(I32),
+                                k_scales[0, 4 * quad : 4 * quad + 4, :].bitcast(I32))
+        nc.scalar.dma_start(lse_rows[0:BLOCKS, :], ls[0, 0].rearrange("(j m) -> j m", m=P))
+        slot_scale = tile([P, PACK], F32, "slot_scale")
+        nc.scalar.dma_start(slot_scale[:], us[0].rearrange("(s r) one -> s (r one)", r=PACK))
+
+        q_rows = qT[0].rearrange("(p r) q -> p r q", r=PACK)
+        q_raw = []
+        for h in range(2):
+            raw = tile([P, PACK, HALF], F32, "q_raw%d" % h)
+            nc.sync.dma_start(raw[:], q_rows[:, :, h * HALF : (h + 1) * HALF])
+            q_raw.append(raw)
+        v_rows = vT.rearrange("(p t) n -> t p n", t=PACK)
+        v_pool = []
+        for t in range(PACK):
+            pool_t = tile([P, TOKENS], F32, "v_pool%d" % t)
+            nc.sync.dma_start(pool_t[:], v_rows[t])
+            v_pool.append(pool_t)
+
+        identity = tile([P, P], F32, "identity")
+        make_identity(nc, identity[:])
+
+        lse_turned = turn.tile([P, P], F32, name="lse_turned", tag="turned")
+        nc.tensor.transpose(lse_turned[:], lse_rows[:], identity[:])
+        neg_lse = tile([P, BLOCKS], F32, "neg_lse")
+        nc.scalar.activation(neg_lse[:], lse_turned[:, 0:BLOCKS], ACT.Copy, scale=-1.0)
+
+        scale_rows = acc.tile([P, PACK, P], F32, name="scale_rows", tag="scale_rows")
+        for r in range(PACK):
+            nc.tensor.transpose(scale_rows[:, r, :], slot_scale[:, r : r + 1].to_broadcast([P, P]), identity[:])
+
+        key_scales = tile([P, SLOTS], U8, "key_scales")
+        nc.vector.tensor_copy(key_scales[:], key_scale_pool[:].indirect(offsets[:]))
+        key_words = tile([P, SLOTS], U32, "key_words")
+        nc.vector.tensor_copy(key_words[:], key_word_pool[:].bitcast(U32).indirect(offsets[:]))
+
+        y_values = tile([P, QUERIES * PACK], BF16, "y_values")
+        for h in range(2):
+            q_values = tile([P, HALF * PACK], BF16, "q_values%d" % h)
+            nc.vector.tensor_copy(q_values[:].rearrange("p (c i r) -> p c r i", i=4, r=PACK),
+                                  q_raw[h][:].rearrange("p r (c i) -> p c r i", i=4))
+            q_codes = tile([P, HALF], U32, "q_codes%d" % h)
+            q_scales = tile([P, HALF], U8, "q_scales%d" % h)
+            quantize(q_codes[:], q_scales[:], q_values[:])
+            for jj in range(2):
+                j = 2 * h + jj
+                cols = slice(jj * P, (jj + 1) * P)
+                scores = acc.tile([P, SLOTS], F32, name="scores%d" % j, tag="bank%d" % j)
+                product(scores[:], q_codes[:, cols], q_scales[:, cols], key_words[:], key_scales[:])
+                weights = tile([P, 2, P, 2], F32, "weights%d" % j, {0: "stage0", 3: "stage1"}.get(j))
+                nc.scalar.activation(weights[:], scores[:].rearrange("p (s u e) -> p u s e", u=2, e=2), ACT.Exp,
+                                     bias=neg_lse[:, j : j + 1])
+                y_rows = tile([P, 2, P, 2], BF16, "y_rows%d" % j, "v_pool0" if j == 1 else None)
+                nc.vector.tensor_tensor(y_rows[:], weights[:],
+                                        scale_rows[:].rearrange("p (u e) s -> p u s e", e=2), ALU.mult)
+                y_pairs = y_rows[:].rearrange("p u s e -> p (u s e)").bitcast(F32)
+                y_turned = turn.tile([P, 2, P], F32, name="y_turned", tag="turned")
+                for u in range(2):
+                    nc.tensor.transpose(y_turned[:, u, :], y_pairs[:, u * P : (u + 1) * P], identity[:])
+                nc.scalar.copy(
+                    y_values[:, j * P * PACK : (j + 1) * P * PACK].bitcast(F32).rearrange("p (m u) -> p m u", u=2),
+                    y_turned[:].rearrange("p u m -> p m u"))
+        y_codes = tile([P, QUERIES], U32, "y_codes", "v_pool1")
+        y_scales = tile([P, QUERIES], U8, "y_scales")
+        quantize(y_codes[:], y_scales[:], y_values[:])
+
+        v_codes, v_scales = [], []
+        for t in range(PACK):
+            v_listed = tile([P, SLOTS], BF16, "v_listed%d" % t, "stage%d" % t)
+            nc.vector.tensor_copy(v_listed[:], v_pool[t][:].indirect(offsets[:]))
+            pairs = v_listed[:].bitcast(F32)
+            v_turned = turn.tile([P, 2, P], F32, name="v_turned", tag="turned")
+            for u in range(2):
+                nc.tensor.transpose(v_turned[:, u, :], pairs[:, u : 2 * P : 2], identity[:])
+            v_values = tile([P, P * PACK], BF16, "v_values%d" % t, {1: "stage2", 2: "stage4"}.get(t))
+            nc.scalar.copy(v_values[:].bitcast(F32).rearrange("p (e u) -> p e u", u=2),
+                           v_turned[:].rearrange("p u e -> p e u"))
+            v_codes.append(tile([P, P], U32, "v_codes%d" % t, "v_pool3" if t == 2 else None))
+            v_scales.append(tile([P, P], U8, "v_scales%d" % t))
+            quantize(v_codes[t][:], v_scales[t][:], v_values[:])
+
+        out_rows = out_0.rearrange("(p t) q -> t p q", t=PACK)
+        out_tile = tile([P, PACK, QUERIES], F32, "out_tile")
+        out_values = tile([P, QUERIES, PACK], BF16, "out_values")
+        for t in range(PACK - 1):
+            result = acc.tile([P, QUERIES], F32, name="result%d" % t, tag="bank%d" % t)
+            product(result[:], v_codes[t][:], v_scales[t][:], y_codes[:], y_scales[:])
+            nc.scalar.copy(out_tile[:, t, :], result[:])
+            nc.sync.dma_start(out_rows[t], out_tile[:, t, :])
+        t = PACK - 1
+        for h in range(2):
+            cols = slice(h * HALF, (h + 1) * HALF)
+            result = acc.tile([P, HALF], F32, name="result_last%d" % h, tag=("bank3", "scale_rows")[h])
+            product(result[:], v_codes[t][:], v_scales[t][:], y_codes[:, cols], y_scales[:, cols])
+            nc.scalar.copy(out_tile[:, t, cols], result[:])
+        nc.sync.dma_start(out_rows[t], out_tile[:, t, :])
+
+        def interleave(engine_copy, lo, hi):
+            engine_copy(out_values[:, lo:hi, :].rearrange("p (c i) t -> p c t i", i=4),
+                        out_tile[:, :, lo:hi].rearrange("p t (c i) -> p c t i", i=4))
+
+        interleave(nc.vector.tensor_copy, 0, HALF)
+        interleave(nc.vector.tensor_copy, HALF, 384)
+        interleave(nc.scalar.copy, 384, QUERIES)
+
+        out_codes = tile([P, QUERIES], U32, "out_codes")
+        out_scales = tile([P, QUERIES], U8, "out_scales")
+        word_rows = out_1[0].rearrange("p q u -> p (q u)").bitcast(I32)
+        for h in range(2):
+            cols = slice(h * HALF, (h + 1) * HALF)
+            quantize(out_codes[:, cols], out_scales[:, cols], out_values[:, cols, :].rearrange("p q t -> p (q t)"))
+            nc.sync.dma_start(word_rows[:, cols], out_codes[:, cols].bitcast(I32))
+        for quad in range(4):
+            queue = nc.sync if quad % 2 else nc.scalar
+            queue.dma_start(out_2[0, 4 * quad : 4 * quad + 4, :].bitcast(I32),
+                            out_scales[32 * quad : 32 * quad + 4, :].bitcast(I32))

@@ -45,25 +45,22 @@ def tile_attend_plo_lse_topk_kernel(tc, qT, k_words, k_scales, vT, ls, us, offs,
         nc.sync.dma_start(offsets[:], offs)
 
         key_scale_pool = tile([P, TOKENS], U8, "key_scale_pool")
-        nc.vector.memset(key_scale_pool[:].bitcast(I32), 0)
+        nc.gpsimd.memset(key_scale_pool[:].bitcast(I32), 0)
         lse_rows = tile([P, P], F32, "lse_rows")
         nc.vector.memset(lse_rows[:], 0.0)
 
+        q_rows = qT[0].rearrange("(p r) q -> p r q", r=PACK)
+        q_raw = [tile([P, PACK, HALF], F32, "q_raw%d" % h) for h in range(2)]
+        nc.sync.dma_start(q_raw[0][:], q_rows[:, :, 0:HALF])
+        for quad in range(4):
+            nc.sync.dma_start(key_scale_pool[32 * quad : 32 * quad + 4, :].bitcast(I32),
+                              k_scales[0, 4 * quad : 4 * quad + 4, :].bitcast(I32))
+        nc.sync.dma_start(lse_rows[0:BLOCKS, :], ls[0, 0].rearrange("(j m) -> j m", m=P))
         key_word_pool = tile([P, TOKENS], I32, "key_word_pool")
         nc.sync.dma_start(key_word_pool[:], k_words[0].rearrange("p n r -> p (n r)").bitcast(I32))
-        for quad in range(4):
-            nc.scalar.dma_start(key_scale_pool[32 * quad : 32 * quad + 4, :].bitcast(I32),
-                                k_scales[0, 4 * quad : 4 * quad + 4, :].bitcast(I32))
-        nc.scalar.dma_start(lse_rows[0:BLOCKS, :], ls[0, 0].rearrange("(j m) -> j m", m=P))
         slot_scale = tile([P, PACK], F32, "slot_scale")
-        nc.scalar.dma_start(slot_scale[:], us[0].rearrange("(s r) one -> s (r one)", r=PACK))
-
-        q_rows = qT[0].rearrange("(p r) q -> p r q", r=PACK)
-        q_raw = []
-        for h in range(2):
-            raw = tile([P, PACK, HALF], F32, "q_raw%d" % h)
-            nc.sync.dma_start(raw[:], q_rows[:, :, h * HALF : (h + 1) * HALF])
-            q_raw.append(raw)
+        nc.sync.dma_start(slot_scale[:], us[0].rearrange("(s r) one -> s (r one)", r=PACK))
+        nc.sync.dma_start(q_raw[1][:], q_rows[:, :, HALF:QUERIES])
         v_rows = vT.rearrange("(p t) n -> t p n", t=PACK)
         v_pool = []
         for t in range(PACK):
@@ -83,10 +80,10 @@ def tile_attend_plo_lse_topk_kernel(tc, qT, k_words, k_scales, vT, ls, us, offs,
         for r in range(PACK):
             nc.tensor.transpose(scale_rows[:, r, :], slot_scale[:, r : r + 1].to_broadcast([P, P]), identity[:])
 
-        key_scales = tile([P, SLOTS], U8, "key_scales")
-        nc.vector.tensor_copy(key_scales[:], key_scale_pool[:].indirect(offsets[:]))
         key_words = tile([P, SLOTS], U32, "key_words")
         nc.vector.tensor_copy(key_words[:], key_word_pool[:].bitcast(U32).indirect(offsets[:]))
+        key_scales = tile([P, SLOTS], U8, "key_scales")
+        nc.vector.tensor_copy(key_scales[:], key_scale_pool[:].indirect(offsets[:]))
 
         y_values = tile([P, QUERIES * PACK], BF16, "y_values")
         for h in range(2):
@@ -101,10 +98,10 @@ def tile_attend_plo_lse_topk_kernel(tc, qT, k_words, k_scales, vT, ls, us, offs,
                 cols = slice(jj * P, (jj + 1) * P)
                 scores = acc.tile([P, SLOTS], F32, name="scores%d" % j, tag="bank%d" % j)
                 product(scores[:], q_codes[:, cols], q_scales[:, cols], key_words[:], key_scales[:])
-                weights = tile([P, 2, P, 2], F32, "weights%d" % j, {0: "stage0", 3: "stage1"}.get(j))
+                weights = tile([P, 2, P, 2], F32, "weights%d" % j)
                 nc.scalar.activation(weights[:], scores[:].rearrange("p (s u e) -> p u s e", u=2, e=2), ACT.Exp,
                                      bias=neg_lse[:, j : j + 1])
-                y_rows = tile([P, 2, P, 2], BF16, "y_rows%d" % j, "v_pool0" if j == 1 else None)
+                y_rows = tile([P, 2, P, 2], BF16, "y_rows%d" % j, "v_pool0" if j == 0 else None)
                 nc.vector.tensor_tensor(y_rows[:], weights[:],
                                         scale_rows[:].rearrange("p (u e) s -> p u s e", e=2), ALU.mult)
                 y_pairs = y_rows[:].rearrange("p u s e -> p (u s e)").bitcast(F32)
@@ -120,16 +117,16 @@ def tile_attend_plo_lse_topk_kernel(tc, qT, k_words, k_scales, vT, ls, us, offs,
 
         v_codes, v_scales = [], []
         for t in range(PACK):
-            v_listed = tile([P, SLOTS], BF16, "v_listed%d" % t, "stage%d" % t)
+            v_listed = tile([P, SLOTS], BF16, "v_listed%d" % t)
             nc.vector.tensor_copy(v_listed[:], v_pool[t][:].indirect(offsets[:]))
             pairs = v_listed[:].bitcast(F32)
             v_turned = turn.tile([P, 2, P], F32, name="v_turned", tag="turned")
             for u in range(2):
                 nc.tensor.transpose(v_turned[:, u, :], pairs[:, u : 2 * P : 2], identity[:])
-            v_values = tile([P, P * PACK], BF16, "v_values%d" % t, {1: "stage2", 2: "stage4"}.get(t))
+            v_values = tile([P, P * PACK], BF16, "v_values%d" % t)
             nc.scalar.copy(v_values[:].bitcast(F32).rearrange("p (e u) -> p e u", u=2),
                            v_turned[:].rearrange("p u e -> p e u"))
-            v_codes.append(tile([P, P], U32, "v_codes%d" % t, "v_pool3" if t == 2 else None))
+            v_codes.append(tile([P, P], U32, "v_codes%d" % t, {1: "v_pool2", 2: "v_pool3"}.get(t)))
             v_scales.append(tile([P, P], U8, "v_scales%d" % t))
             quantize(v_codes[t][:], v_scales[t][:], v_values[:])
 
@@ -147,7 +144,7 @@ def tile_attend_plo_lse_topk_kernel(tc, qT, k_words, k_scales, vT, ls, us, offs,
             result = acc.tile([P, HALF], F32, name="result_last%d" % h, tag=("bank3", "scale_rows")[h])
             product(result[:], v_codes[t][:], v_scales[t][:], y_codes[:, cols], y_scales[:, cols])
             nc.scalar.copy(out_tile[:, t, cols], result[:])
-        nc.sync.dma_start(out_rows[t], out_tile[:, t, :])
+            nc.sync.dma_start(out_rows[t][:, cols], out_tile[:, t, cols])
 
         def interleave(engine_copy, lo, hi):
             engine_copy(out_values[:, lo:hi, :].rearrange("p (c i) t -> p c t i", i=4),

@@ -101,7 +101,7 @@ def tile_attend_plo_lse_topk_kernel(tc, qT, k_words, k_scales, vT, ls, us, offs,
                 weights = tile([P, 2, P, 2], F32, "weights%d" % j)
                 nc.scalar.activation(weights[:], scores[:].rearrange("p (s u e) -> p u s e", u=2, e=2), ACT.Exp,
                                      bias=neg_lse[:, j : j + 1])
-                y_rows = tile([P, 2, P, 2], BF16, "y_rows%d" % j, "v_pool0" if j == 0 else None)
+                y_rows = tile([P, 2, P, 2], BF16, "y_rows%d" % j, "v_pool0" if j == 1 else None)
                 nc.vector.tensor_tensor(y_rows[:], weights[:],
                                         scale_rows[:].rearrange("p (u e) s -> p u s e", e=2), ALU.mult)
                 y_pairs = y_rows[:].rearrange("p u s e -> p (u s e)").bitcast(F32)
@@ -123,7 +123,7 @@ def tile_attend_plo_lse_topk_kernel(tc, qT, k_words, k_scales, vT, ls, us, offs,
             v_turned = turn.tile([P, 2, P], F32, name="v_turned", tag="turned")
             for u in range(2):
                 nc.tensor.transpose(v_turned[:, u, :], pairs[:, u : 2 * P : 2], identity[:])
-            v_values = tile([P, P * PACK], BF16, "v_values%d" % t)
+            v_values = tile([P, P * PACK], BF16, "v_values%d" % t, "stage4" if t == 3 else None)
             nc.scalar.copy(v_values[:].bitcast(F32).rearrange("p (e u) -> p e u", u=2),
                            v_turned[:].rearrange("p u e -> p e u"))
             v_codes.append(tile([P, P], U32, "v_codes%d" % t, {1: "v_pool2", 2: "v_pool3"}.get(t)))
@@ -132,12 +132,14 @@ def tile_attend_plo_lse_topk_kernel(tc, qT, k_words, k_scales, vT, ls, us, offs,
 
         out_rows = out_0.rearrange("(p t) q -> t p q", t=PACK)
         out_tile = tile([P, PACK, QUERIES], F32, "out_tile")
-        out_values = tile([P, QUERIES, PACK], BF16, "out_values")
+        out_values = tile([P, QUERIES, PACK], BF16, "out_values", "stage4")
         for t in range(PACK - 1):
             result = acc.tile([P, QUERIES], F32, name="result%d" % t, tag="bank%d" % t)
             product(result[:], v_codes[t][:], v_scales[t][:], y_codes[:], y_scales[:])
             nc.scalar.copy(out_tile[:, t, :], result[:])
             nc.sync.dma_start(out_rows[t], out_tile[:, t, :])
+            if t == 1:
+                nc.vector.tensor_copy(out_values[:, :, 0:2], out_tile[:, 0:2, :].rearrange("p t q -> p q t"))
         t = PACK - 1
         for h in range(2):
             cols = slice(h * HALF, (h + 1) * HALF)
@@ -146,13 +148,9 @@ def tile_attend_plo_lse_topk_kernel(tc, qT, k_words, k_scales, vT, ls, us, offs,
             nc.scalar.copy(out_tile[:, t, cols], result[:])
             nc.sync.dma_start(out_rows[t][:, cols], out_tile[:, t, cols])
 
-        def interleave(engine_copy, lo, hi):
-            engine_copy(out_values[:, lo:hi, :].rearrange("p (c i) t -> p c t i", i=4),
-                        out_tile[:, :, lo:hi].rearrange("p t (c i) -> p c t i", i=4))
-
-        interleave(nc.vector.tensor_copy, 0, HALF)
-        interleave(nc.vector.tensor_copy, HALF, 384)
-        interleave(nc.scalar.copy, 384, QUERIES)
+        for h in range(2):
+            cols = slice(h * HALF, (h + 1) * HALF)
+            nc.vector.tensor_copy(out_values[:, cols, 2:4], out_tile[:, 2:4, cols].rearrange("p t q -> p q t"))
 
         out_codes = tile([P, QUERIES], U32, "out_codes")
         out_scales = tile([P, QUERIES], U8, "out_scales")

from contextlib import ExitStack

import concourse.mybir as mybir
from concourse.masks import make_identity

F32 = mybir.dt.float32
BF16 = mybir.dt.bfloat16
I32 = mybir.dt.int32
U32 = mybir.dt.uint32
U16 = mybir.dt.uint16
U8 = mybir.dt.uint8
FP8X4 = mybir.dt.float8_e4m3fn_x4
ACT = mybir.ActivationFunctionType
ALU = mybir.AluOpType

P = 128
PACK = 4
SLOTS = 512
TOKENS = 2048
QUERIES = 512
HALF = QUERIES // 2
BLOCKS = QUERIES // P

FLOPS = 2 * 2 * 512 * 512 * 512


def tile_attend_plo_lse_topk_kernel(tc, qT, k_words, k_scales, vT, ls, us, offs, out_0, out_1, out_2):
    nc = tc.nc
    with ExitStack() as ctx:
        sb = ctx.enter_context(tc.tile_pool(name="sb", bufs=1))
        acc = ctx.enter_context(tc.psum_pool(name="acc", bufs=1))
        turn = ctx.enter_context(tc.psum_pool(name="turn", bufs=3))

        def tile(shape, dtype, name, tag=None):
            return sb.tile(shape, dtype, name=name, tag=tag or name, align_bytes=64)

        def quantize(codes, scales, values):
            nc.vector.quantize_mx(out=codes.bitcast(FP8X4), scales=scales, in_=values)

        def product(out, lhs_codes, lhs_scales, rhs_codes, rhs_scales):
            nc.tensor.matmul_mx(out=out, lhsT=lhs_codes.bitcast(FP8X4), lhsT_scale=lhs_scales,
                                rhs=rhs_codes.bitcast(FP8X4), rhs_scale=rhs_scales, start=True, stop=True)

        offsets = sb.tile([P, SLOTS // 16], U16, name="offsets")
        nc.sync.dma_start(offsets[:], offs)

        key_scale_pool = tile([P, TOKENS], U8, "key_scale_pool")
        nc.gpsimd.memset(key_scale_pool[:].bitcast(I32), 0)
        lse_rows = tile([P, P], F32, "lse_rows")
        nc.vector.memset(lse_rows[:], 0.0)

        q_rows = qT[0].rearrange("(p r) q -> p r q", r=PACK)
        q_raw = [tile([P, PACK, HALF], F32, "q_raw%d" % h) for h in range(2)]
        nc.sync.dma_start(q_raw[0][:], q_rows[:, :, 0:HALF])
        for quad in range(4):
            nc.sync.dma_start(key_scale_pool[32 * quad : 32 * quad + 4, :].bitcast(I32),
                              k_scales[0, 4 * quad : 4 * quad + 4, :].bitcast(I32))
        nc.sync.dma_start(lse_rows[0:BLOCKS, :], ls[0, 0].rearrange("(j m) -> j m", m=P))
        key_word_pool = tile([P, TOKENS], I32, "key_word_pool")
        nc.sync.dma_start(key_word_pool[:], k_words[0].rearrange("p n r -> p (n r)").bitcast(I32))
        slot_scale = tile([P, PACK], F32, "slot_scale")
        nc.sync.dma_start(slot_scale[:], us[0].rearrange("(s r) one -> s (r one)", r=PACK))
        nc.sync.dma_start(q_raw[1][:], q_rows[:, :, HALF:QUERIES])
        v_rows = vT.rearrange("(p t) n -> t p n", t=PACK)
        v_pool = []
        for t in range(PACK):
            pool_t = tile([P, TOKENS], F32, "v_pool%d" % t)
            nc.sync.dma_start(pool_t[:], v_rows[t])
            v_pool.append(pool_t)

        identity = tile([P, P], F32, "identity")
        make_identity(nc, identity[:])

        lse_turned = turn.tile([P, P], F32, name="lse_turned", tag="turned")
        nc.tensor.transpose(lse_turned[:], lse_rows[:], identity[:])
        neg_lse = tile([P, BLOCKS], F32, "neg_lse")
        nc.scalar.activation(neg_lse[:], lse_turned[:, 0:BLOCKS], ACT.Copy, scale=-1.0)

        scale_rows = acc.tile([P, PACK, P], F32, name="scale_rows", tag="scale_rows")
        for r in range(PACK):
            nc.tensor.transpose(scale_rows[:, r, :], slot_scale[:, r : r + 1].to_broadcast([P, P]), identity[:])

        key_words = tile([P, SLOTS], U32, "key_words")
        nc.vector.tensor_copy(key_words[:], key_word_pool[:].bitcast(U32).indirect(offsets[:]))
        key_scales = tile([P, SLOTS], U8, "key_scales")
        nc.vector.tensor_copy(key_scales[:], key_scale_pool[:].indirect(offsets[:]))

        y_values = tile([P, QUERIES * PACK], BF16, "y_values")
        for h in range(2):
            q_values = tile([P, HALF * PACK], BF16, "q_values%d" % h)
            nc.vector.tensor_copy(q_values[:].rearrange("p (c i r) -> p c r i", i=4, r=PACK),
                                  q_raw[h][:].rearrange("p r (c i) -> p c r i", i=4))
            q_codes = tile([P, HALF], U32, "q_codes%d" % h)
            q_scales = tile([P, HALF], U8, "q_scales%d" % h)
            quantize(q_codes[:], q_scales[:], q_values[:])
            for jj in range(2):
                j = 2 * h + jj
                cols = slice(jj * P, (jj + 1) * P)
                scores = acc.tile([P, SLOTS], F32, name="scores%d" % j, tag="bank%d" % j)
                product(scores[:], q_codes[:, cols], q_scales[:, cols], key_words[:], key_scales[:])
                weights = tile([P, 2, P, 2], F32, "weights%d" % j)
                nc.scalar.activation(weights[:], scores[:].rearrange("p (s u e) -> p u s e", u=2, e=2), ACT.Exp,
                                     bias=neg_lse[:, j : j + 1])
                y_rows = tile([P, 2, P, 2], BF16, "y_rows%d" % j, "v_pool0" if j == 1 else None)
                nc.vector.tensor_tensor(y_rows[:], weights[:],
                                        scale_rows[:].rearrange("p (u e) s -> p u s e", e=2), ALU.mult)
                y_pairs = y_rows[:].rearrange("p u s e -> p (u s e)").bitcast(F32)
                y_turned = turn.tile([P, 2, P], F32, name="y_turned", tag="turned")
                for u in range(2):
                    nc.tensor.transpose(y_turned[:, u, :], y_pairs[:, u * P : (u + 1) * P], identity[:])
                nc.scalar.copy(
                    y_values[:, j * P * PACK : (j + 1) * P * PACK].bitcast(F32).rearrange("p (m u) -> p m u", u=2),
                    y_turned[:].rearrange("p u m -> p m u"))
        y_codes = tile([P, QUERIES], U32, "y_codes", "v_pool1")
        y_scales = tile([P, QUERIES], U8, "y_scales")
        quantize(y_codes[:], y_scales[:], y_values[:])

        v_codes, v_scales = [], []
        for t in range(PACK):
            v_listed = tile([P, SLOTS], BF16, "v_listed%d" % t)
            nc.vector.tensor_copy(v_listed[:], v_pool[t][:].indirect(offsets[:]))
            pairs = v_listed[:].bitcast(F32)
            v_turned = turn.tile([P, 2, P], F32, name="v_turned", tag="turned")
            for u in range(2):
                nc.tensor.transpose(v_turned[:, u, :], pairs[:, u : 2 * P : 2], identity[:])
            v_values = tile([P, P * PACK], BF16, "v_values%d" % t, "stage4" if t == 3 else None)
            nc.scalar.copy(v_values[:].bitcast(F32).rearrange("p (e u) -> p e u", u=2),
                           v_turned[:].rearrange("p u e -> p e u"))
            v_codes.append(tile([P, P], U32, "v_codes%d" % t, {1: "v_pool2", 2: "v_pool3"}.get(t)))
            v_scales.append(tile([P, P], U8, "v_scales%d" % t))
            quantize(v_codes[t][:], v_scales[t][:], v_values[:])

        out_rows = out_0.rearrange("(p t) q -> t p q", t=PACK)
        out_tile = tile([P, PACK, QUERIES], F32, "out_tile")
        out_values = tile([P, QUERIES, PACK], BF16, "out_values", "stage4")
        for t in range(PACK - 1):
            result = acc.tile([P, QUERIES], F32, name="result%d" % t, tag="bank%d" % t)
            product(result[:], v_codes[t][:], v_scales[t][:], y_codes[:], y_scales[:])
            nc.scalar.copy(out_tile[:, t, :], result[:])
            nc.sync.dma_start(out_rows[t], out_tile[:, t, :])
            if t == 1:
                nc.vector.tensor_copy(out_values[:, :, 0:2], out_tile[:, 0:2, :].rearrange("p t q -> p q t"))
        t = PACK - 1
        for h in range(2):
            cols = slice(h * HALF, (h + 1) * HALF)
            result = acc.tile([P, HALF], F32, name="result_last%d" % h, tag=("bank3", "scale_rows")[h])
            product(result[:], v_codes[t][:], v_scales[t][:], y_codes[:, cols], y_scales[:, cols])
            nc.scalar.copy(out_tile[:, t, cols], result[:])
            nc.sync.dma_start(out_rows[t][:, cols], out_tile[:, t, cols])

        for h in range(2):
            cols = slice(h * HALF, (h + 1) * HALF)
            nc.vector.tensor_copy(out_values[:, cols, 2:4], out_tile[:, 2:4, cols].rearrange("p t q -> p q t"))

        out_codes = tile([P, QUERIES], U32, "out_codes")
        out_scales = tile([P, QUERIES], U8, "out_scales")
        word_rows = out_1[0].rearrange("p q u -> p (q u)").bitcast(I32)
        for h in range(2):
            cols = slice(h * HALF, (h + 1) * HALF)
            quantize(out_codes[:, cols], out_scales[:, cols], out_values[:, cols, :].rearrange("p q t -> p (q t)"))
            nc.sync.dma_start(word_rows[:, cols], out_codes[:, cols].bitcast(I32))
        for quad in range(4):
            queue = nc.sync if quad % 2 else nc.scalar
            queue.dma_start(out_2[0, 4 * quad : 4 * quad + 4, :].bitcast(I32),
                            out_scales[32 * quad : 32 * quad + 4, :].bitcast(I32))
